import numpy as np
import ml_dtypes


def mxq(x, axis, fmt="e4m3"):
    dtype, down = {"e4m3": (ml_dtypes.float8_e4m3fn, 7), "e5m2": (ml_dtypes.float8_e5m2, 14)}[fmt]
    v = np.moveaxis(np.asarray(x, np.float32).astype(ml_dtypes.bfloat16).astype(np.float64), axis, -1)
    blocks = v.reshape(v.shape[:-1] + (-1, 32))
    amax = np.abs(blocks).max(-1, keepdims=True)
    byte = np.maximum(np.where(amax > 0, np.frexp(amax)[1] - 1 + 127, 0) - down, 1)
    scale = np.exp2(byte - 127.0)
    codes = (blocks / scale).astype(np.float32).astype(dtype).astype(np.float64)
    return np.moveaxis((codes * scale).reshape(v.shape), -1, axis)


WIDE = False


def mx_kscale(k):
    if not WIDE:
        return np.ones(k)
    levels = np.array([10, -10, 5, -5, 0])
    if k % 512:
        return np.exp2(np.random.permutation(np.resize(levels, k // 32))).repeat(32)
    a = np.empty((k // 512, 16))
    for p in range(k // 512):
        a[p, :8] = np.random.permutation(np.resize(levels, 8))
        for g in range(8):
            far = levels[np.abs(levels - a[p, g]) >= 10]
            a[p, g + 8] = far[np.random.randint(len(far))]
    return np.exp2(a.ravel()).repeat(32)


BF16 = ml_dtypes.bfloat16


def bf(x):
    return np.asarray(x, np.float32).astype(BF16)


def f64(x):
    return np.asarray(x).astype(np.float64)


E2M1 = np.array([0.0, 0.5, 1.0, 1.5, 2.0, 3.0, 4.0, 6.0, -0.0, -0.5, -1.0, -1.5, -2.0, -3.0, -4.0, -6.0])


def pack_weight(w, fmt):
    k, n = w.shape
    w = f64(bf(w)).reshape(k // 32, 32, n)
    amax = np.abs(w).max(1)
    if fmt == "e4m3":
        byte = np.frexp(amax)[1] - 1 + 127 - 7
    else:
        mant, ex = np.frexp(amax / 6.0)
        byte = np.where(mant > 0.5, ex, ex - 1) + 127
    byte = np.clip(np.where(amax > 0, byte, 1), 1, 254)
    scaled = (w * np.exp2(127.0 - byte)[:, None, :]).reshape(k, n).astype(np.float32)
    by_word = np.ascontiguousarray(scaled.reshape(k // 512, 128, 4, n).transpose(0, 1, 3, 2))
    if fmt == "e4m3":
        words = by_word.astype(ml_dtypes.float8_e4m3fn).view(np.uint8)
    else:
        c = by_word.astype(ml_dtypes.float4_e2m1fn).view(np.uint8) & 0xF
        words = c[..., 0::2] | (c[..., 1::2] << 4)
    return np.ascontiguousarray(words), np.ascontiguousarray(byte.astype(np.uint8).reshape(k // 512, 16, n))


def unpack_weight(words, scales, fmt):
    g, p, n, _ = words.shape
    if fmt == "e4m3":
        vals = np.ascontiguousarray(words).view(ml_dtypes.float8_e4m3fn).astype(np.float64)
    else:
        nib = np.empty((g, p, n, 4), np.uint8)
        nib[..., 0::2] = words & 0xF
        nib[..., 1::2] = words >> 4
        vals = E2M1[nib]
    vals = vals * np.repeat(np.exp2(scales.astype(np.float64) - 127.0), 8, axis=1)[..., None]
    return vals.transpose(0, 1, 3, 2).reshape(g * 512, n)
def pack4(w):
    words, scales = pack_weight(w, "e2m1")
    return words.reshape(words.shape[0], 128, -1), scales


def unpack4(words, scales):
    return unpack_weight(words.reshape(words.shape[0], 128, -1, 2), scales, "e2m1")


B, N, T, D, E = 2, 1024, 512, 512, 512


def draw0():
    s, u, t = mx_kscale(D), mx_kscale(D), mx_kscale(T)
    v = bf(np.random.standard_normal((B, N, D)) * s)
    q = bf(np.random.standard_normal((B, T, D)) * u)
    wb = bf(np.random.standard_normal(D) / (s * u))
    wv_words, wv_scales = pack4(np.random.standard_normal((D, E)) / np.sqrt(D) / s[:, None])
    wq_words, wq_scales = pack4(np.random.standard_normal((D, E)) / np.sqrt(D) / u[:, None])
    return {
        "v": v,
        "q": q,
        "wb": wb,
        "wv_words": wv_words,
        "wv_scales": wv_scales,
        "wq_words": wq_words,
        "wq_scales": wq_scales,
        "gc": bf((1.0 + 0.1 * np.random.standard_normal(T)) * t),
        "gp": bf((1.0 + 0.1 * np.random.standard_normal(T)) / t),
    }


def core(v, q, wb, wv_words, wv_scales, wq_words, wq_scales, gc, gp):
    vq = mxq(f64(v), 2, "e4m3")
    qb = f64(q) * f64(wb)[None, None, :]
    scores = mxq(qb, 2, "e4m3") @ vq.transpose(0, 2, 1)
    c = np.tanh(scores / np.sqrt(D))
    cg = c * f64(gc)[None, :, None]
    pv = vq @ unpack4(wv_words, wv_scales)
    pq = f64(gp)[None, :, None] * (mxq(f64(q), 2, "e4m3") @ unpack4(wq_words, wq_scales))
    m = (mxq(cg, 1, "e4m3").transpose(0, 2, 1) @ mxq(pq, 1, "e4m3")) / np.sqrt(T)
    return np.tanh(pv + m)


def e4m3fn_bytes(y):
    return np.clip(np.asarray(y, np.float64), -448.0, 448.0).astype(np.float32).astype(ml_dtypes.float8_e4m3fn).view(np.uint8)


def e4m3fn_values(b):
    return np.asarray(b, np.uint8).view(ml_dtypes.float8_e4m3fn).astype(np.float64)


def setup_inputs():
    d = draw0()
    x0 = np.asarray(d['v']).astype(np.float64)
    s = (np.max(np.abs(x0), axis=(0, 1), keepdims=True) / 448.0).astype(np.float32)
    out = {}
    for k, v in d.items():
        if k == 'v':
            out['v_bytes'] = e4m3fn_bytes(x0 / s.astype(np.float64))
            out['v_scale'] = s
        else:
            out[k] = v
    return out


def reference(v_bytes, v_scale, q, wb, wv_words, wv_scales, wq_words, wq_scales, gc, gp):
    return core(e4m3fn_values(v_bytes) * v_scale.astype(np.float64), q, wb, wv_words, wv_scales, wq_words, wq_scales, gc, gp)

@@ -1,0 +1,322 @@
+import math
+from contextlib import ExitStack
+
+import concourse.mybir as mybir
+from concourse.masks import make_identity
+
+B, N, T, D, E = 2, 1024, 512, 512, 512
+FLOPS = 2 * B * (T * N * D + N * D * E + T * D * E + N * T * E)
+
+F32 = mybir.dt.float32
+BF16 = mybir.dt.bfloat16
+U8 = mybir.dt.uint8
+U32 = mybir.dt.uint32
+I32 = mybir.dt.int32
+FP8 = mybir.dt.float8_e4m3fn
+FP8X4 = mybir.dt.float8_e4m3fn_x4
+FP4X4 = mybir.dt.float4_e2m1fn_x4
+MULT = mybir.AluOpType.mult
+ADD = mybir.AluOpType.add
+TANH = mybir.ActivationFunctionType.Tanh
+COPY = mybir.ActivationFunctionType.Copy
+
+P = 128
+PACK = 4
+ROWS = N // P
+PAIRS = ROWS // 2
+STEPS = B * PAIRS
+
+
+def tile_coattentionaffinityimageside_w4_kernel(
+    tc, v_bytes, v_scale, q, wb, wv_words, wv_scales, wq_words, wq_scales, gc, gp, out
+):
+    nc = tc.nc
+    with ExitStack() as ctx:
+        keep = ctx.enter_context(tc.tile_pool(name="keep", bufs=1))
+        work = ctx.enter_context(tc.tile_pool(name="work", bufs=3))
+        psum = ctx.enter_context(tc.psum_pool(name="psum", bufs=2))
+        ctx.enter_context(tc.manual_schedule())
+
+        ident = keep.tile([P, P], F32, name="ident")
+        make_identity(nc, ident[:])
+        warm = keep.tile([P, 8], F32, name="warm")
+        nc.vector.memset(warm[:], 0.0)
+        warm_out = keep.tile([P, 8], F32, name="warm_out")
+        nc.scalar.activation(out=warm_out[:], in_=warm[:], func=TANH)
+
+        w_codes = {}
+        w_scale = {}
+        for name in ("wq", "wv"):
+            w_scale[name] = keep.tile([P, E], U8, name=name + "_scale", align_bytes=64)
+            nc.vector.memset(w_scale[name][:].bitcast(I32), 0)
+
+        def load_vector(name, vec, dtype):
+            col = keep.tile([P, PACK], dtype, name=name)
+            nc.sync.dma_start(out=col[:], in_=vec.rearrange("(p j) -> p j", j=PACK))
+            return col
+
+        def load_weight(name, words, scales):
+            w_codes[name] = keep.tile([P, 2 * E], U8, name=name + "_codes", align_bytes=64)
+            nc.sync.dma_start(out=w_codes[name][:].bitcast(I32), in_=words[0].bitcast(I32))
+            for r in range(4):
+                nc.sync.dma_start(
+                    out=w_scale[name][r:P:32, :].bitcast(I32), in_=scales[0, r:16:4, :].bitcast(I32)
+                )
+
+        q_rows = {}
+
+        def load_q(b, h):
+            q_rows[b, h] = keep.tile([P, 2 * D], BF16, name="q_rows_%d_%d" % (b, h))
+            src = q[b].rearrange("(m j) k -> m (j k)", j=PACK)
+            nc.sync.dma_start(out=q_rows[b, h][:], in_=src[:, 2 * D * h : 2 * D * (h + 1)])
+
+        v_raw = {}
+
+        def load_v(b, g0, g1):
+            raw = keep.tile([P, 2 * D * (g1 - g0)], U8, name="v_raw_%d_%d" % (b, g0))
+            src = v_bytes[b].rearrange("(p i) k -> p (i k)", i=ROWS)
+            nc.sync.dma_start(out=raw[:], in_=src[:, 2 * D * g0 : 2 * D * g1])
+            for g in range(g0, g1):
+                v_raw[b * PAIRS + g] = raw[:, 2 * D * (g - g0) : 2 * D * (g - g0 + 1)]
+
+        vs_col = load_vector("vs_col", v_scale.rearrange("a o k -> (a o k)"), F32)
+        load_q(0, 0)
+        load_v(0, 0, 1)
+        load_q(0, 1)
+        wb_col = load_vector("wb_col", wb, BF16)
+        load_v(0, 1, PAIRS)
+        gp_col = load_vector("gp_col", gp, BF16)
+        load_weight("wq", wq_words, wq_scales)
+        gc_col = load_vector("gc_col", gc, BF16)
+        load_weight("wv", wv_words, wv_scales)
+        load_q(1, 0)
+        load_q(1, 1)
+        load_v(1, 0, PAIRS)
+
+        vs_full = keep.tile([P, 2 * D], F32, name="vs_full")
+        spread = psum.tile([P, PACK, P], F32, name="spread", tag="bank", bufs=6)
+        for j in range(PACK):
+            nc.tensor.transpose(spread[:, j, :], vs_col[:, j : j + 1].to_broadcast([P, P]), ident[:])
+        nc.vector.tensor_copy(
+            out=vs_full[:, :D].rearrange("p (m j) -> p m j", j=PACK), in_=spread[:].rearrange("p j m -> p m j")
+        )
+        nc.scalar.copy(
+            out=vs_full[:, D:].rearrange("p (m j) -> p m j", j=PACK), in_=spread[:].rearrange("p j m -> p m j")
+        )
+
+        def turn(rows, grouped):
+            words = rows.bitcast(F32)
+            bank = psum.tile([P, 2, 2, P], F32, name="turned", tag="bank", bufs=6)
+            for a in range(2):
+                for u in range(2):
+                    nc.tensor.transpose(bank[:, a, u, :], words[:, 256 * a + u : 256 * (a + 1) : 2], ident[:])
+            nc.scalar.copy(
+                out=grouped.bitcast(F32).rearrange("p (a r u) -> p a r u", a=2, u=2),
+                in_=bank[:].rearrange("p a u r -> p a r u"),
+            )
+
+        def quantize(name, values, pool, bufs):
+            cols = values.shape[1] // PACK
+            codes = pool.tile([P, cols], U32, name=name + "_codes", bufs=bufs, align_bytes=64)
+            scales = pool.tile([P, cols], U8, name=name + "_scales", bufs=bufs, align_bytes=64)
+            nc.vector.quantize_mx(out=codes[:].bitcast(FP8X4), scales=scales[:], in_=values)
+            return codes, scales
+
+        def product(acc, left, c0, right, r0, width):
+            nc.tensor.matmul_mx(
+                out=acc,
+                lhsT=left[0][:, c0 : c0 + P].bitcast(FP8X4),
+                lhsT_scale=left[1][:, c0 : c0 + P],
+                rhs=right[0][:, r0 : r0 + width].bitcast(FP8X4),
+                rhs_scale=right[1][:, r0 : r0 + width],
+                start=True,
+                stop=True,
+            )
+
+        def project(acc, left, c0, name):
+            nc.tensor.matmul_mx(
+                out=acc,
+                lhsT=left[0][:, c0 : c0 + P].bitcast(FP8X4),
+                lhsT_scale=left[1][:, c0 : c0 + P],
+                rhs=w_codes[name][:].bitcast(FP4X4),
+                rhs_scale=w_scale[name][:],
+                start=True,
+                stop=True,
+            )
+
+        q_grp, qb_grp, q_mx, qb_mx, pq_planes, pq_grp, pq_mx = {}, {}, {}, {}, {}, {}, {}
+        v_wide, v_grp, v_mx, c_val, cg_val, cg_mx, pv_val, m_acc, total = {}, {}, {}, {}, {}, {}, {}, {}, {}
+
+        def turn_q(b, h):
+            if h == 0:
+                q_grp[b] = work.tile([P, PACK * T], BF16, name="q_grp", bufs=1, align_bytes=64)
+            turn(q_rows[b, h][:], q_grp[b][:, 2 * D * h : 2 * D * (h + 1)])
+
+        def scale_q(b):
+            qb_grp[b] = work.tile([P, PACK * T], BF16, name="qb_grp", bufs=1, align_bytes=64)
+            nc.vector.tensor_tensor(
+                out=qb_grp[b][:].rearrange("p (t j) -> p t j", j=PACK),
+                in0=q_grp[b][:].rearrange("p (t j) -> p t j", j=PACK),
+                in1=wb_col[:].unsqueeze(1).to_broadcast([P, T, PACK]),
+                op=MULT,
+            )
+
+        def quant_q(b):
+            q_mx[b] = quantize("q", q_grp[b][:], work, 2)
+
+        def quant_qb(b):
+            qb_mx[b] = quantize("qb", qb_grp[b][:], work, 2)
+
+        def project_q(b, j):
+            if j == 0:
+                pq_planes[b] = work.tile([P, PACK, E], BF16, name="pq_planes", bufs=1)
+            acc = psum.tile([P, E], F32, name="pq_acc", tag="bank", bufs=6)
+            project(acc[:], q_mx[b], P * j, "wq")
+            nc.scalar.activation(out=pq_planes[b][:, j, :], in_=acc[:], func=COPY, scale=gp_f32[:, j : j + 1])
+
+        def group_pq(b):
+            pq_grp[b] = work.tile([P, PACK * E], BF16, name="pq_grp", bufs=1, align_bytes=64)
+            nc.vector.tensor_copy(
+                out=pq_grp[b][:].rearrange("p (c i j) -> p c j i", i=4, j=PACK),
+                in_=pq_planes[b][:].rearrange("p j (c i) -> p c j i", i=4),
+            )
+
+        def quant_pq(b):
+            pq_mx[b] = quantize("pq", pq_grp[b][:], work, 2)
+
+        def widen(s, parts):
+            v_wide[s] = work.tile([P, 2 * D], BF16, name="v_wide")
+            w = 2 * D // parts
+            for i in range(parts):
+                nc.vector.tensor_tensor(
+                    out=v_wide[s][:, w * i : w * (i + 1)],
+                    in0=v_raw[s][:, w * i : w * (i + 1)].bitcast(FP8),
+                    in1=vs_full[:, :w],
+                    op=MULT,
+                )
+
+        def turn_v(s):
+            v_grp[s] = work.tile([P, 2 * D], BF16, name="v_grp", align_bytes=64)
+            turn(v_wide[s][:], v_grp[s][:])
+
+        def quant_v(s):
+            v_mx[s] = quantize("v", v_grp[s][:], work, 3)
+
+        def affinity(s, a):
+            if a == 0:
+                c_val[s] = work.tile([P, 2, P, PACK], F32, name="c_val")
+            acc = psum.tile([P, PACK, P], F32, name="score", tag="bank", bufs=6)
+            for j in range(PACK):
+                product(acc[:, j, :], qb_mx[s // PAIRS], P * j, v_mx[s], P * a, P)
+            nc.scalar.activation(
+                out=c_val[s][:, a, :, :], in_=acc[:].rearrange("p j r -> p r j"), func=TANH, scale=1.0 / math.sqrt(D)
+            )
+
+        def project_v(s, a):
+            if a == 0:
+                pv_val[s] = work.tile([P, 2, E], F32, name="pv_val")
+            acc = psum.tile([P, E], F32, name="pv_acc", tag="bank", bufs=6)
+            project(acc[:], v_mx[s], P * a, "wv")
+            nc.scalar.copy(out=pv_val[s][:, a, :], in_=acc[:])
+
+        def gain(s):
+            cg_val[s] = work.tile([P, 2 * P * PACK], BF16, name="cg_val", align_bytes=64)
+            nc.vector.tensor_tensor(
+                out=cg_val[s][:].rearrange("p (r j) -> p r j", j=PACK),
+                in0=c_val[s][:].rearrange("p a r j -> p (a r) j"),
+                in1=gc_col[:].unsqueeze(1).to_broadcast([P, 2 * P, PACK]),
+                op=MULT,
+            )
+
+        def quant_cg(s):
+            cg_mx[s] = quantize("cg", cg_val[s][:], work, 3)
+
+        def mix(s, a):
+            m_acc[s, a] = psum.tile([P, E], F32, name="m_acc", tag="mix")
+            product(m_acc[s, a][:], cg_mx[s], P * a, pq_mx[s // PAIRS], 0, E)
+
+        def add(s, a):
+            if a == 0:
+                total[s] = work.tile([P, 2, E], F32, name="total")
+            nc.vector.scalar_tensor_tensor(
+                out=total[s][:, a, :], in0=m_acc[s, a][:], scalar=1.0 / math.sqrt(T), in1=pv_val[s][:, a, :],
+                op0=MULT, op1=ADD,
+            )
+
+        def finish(s, a0, a1):
+            res = work.tile([P, a1 - a0, E], F32, name="res", bufs=4)
+            nc.scalar.activation(out=res[:], in_=total[s][:, a0:a1, :], func=TANH)
+            b, g = divmod(s, PAIRS)
+            dst = out[b].rearrange("(p i) e -> p i e", i=ROWS)
+            nc.sync.dma_start(out=dst[:, 2 * g + a0 : 2 * g + a1, :], in_=res[:])
+
+        turn_q(0, 0)
+        widen(0, 2)
+        turn_q(0, 1)
+        turn_v(0)
+        gp_f32 = keep.tile([P, PACK], F32, name="gp_f32")
+        nc.scalar.copy(out=gp_f32[:], in_=gp_col[:])
+        widen(1, 1)
+        quant_q(0)
+        scale_q(0)
+        turn_v(1)
+        quant_v(0)
+        for j in range(2):
+            project_q(0, j)
+        quant_qb(0)
+        widen(2, 1)
+        for j in range(2, 4):
+            project_q(0, j)
+        affinity(0, 0)
+        affinity(0, 1)
+        quant_v(1)
+        widen(3, 1)
+        turn_v(2)
+        group_pq(0)
+        affinity(1, 0)
+        affinity(1, 1)
+
+        for s in range(STEPS + 1):
+            if s + 2 < STEPS:
+                quant_v(s + 2)
+            if s < STEPS:
+                gain(s)
+            if s + 3 < STEPS:
+                turn_v(s + 3)
+            if s == 0:
+                turn_q(1, 0)
+                turn_q(1, 1)
+            if s > 0:
+                add(s - 1, 0)
+            if s % PAIRS == 0 and s < STEPS:
+                quant_pq(s // PAIRS)
+            if s < STEPS:
+                project_v(s, 0)
+                project_v(s, 1)
+                quant_cg(s)
+            if s > 0:
+                add(s - 1, 1)
+            if s + 2 < STEPS:
+                affinity(s + 2, 0)
+                affinity(s + 2, 1)
+            if s in (1, 2):
+                project_q(1, 2 * s - 2)
+                project_q(1, 2 * s - 1)
+            if s == 1:
+                scale_q(1)
+            if s < STEPS:
+                mix(s, 0)
+                mix(s, 1)
+            if s + 4 < STEPS:
+                widen(s + 4, 1)
+            if s == 0:
+                quant_q(1)
+            if s == 1:
+                quant_qb(1)
+            if s == 3:
+                group_pq(1)
+            if 0 < s < STEPS:
+                finish(s - 1, 0, 2)
+            if s == STEPS:
+                finish(s - 1, 0, 1)
+                finish(s - 1, 1, 2)

@@ -25,6 +25,7 @@ PACK = 4
 ROWS = N // P
 PAIRS = ROWS // 2
 STEPS = B * PAIRS
+WHOLE = [(0, 2 * D)]
 
 
 def tile_coattentionaffinityimageside_w4_kernel(
@@ -38,9 +39,10 @@ def tile_coattentionaffinityimageside_w4_kernel(
         ctx.enter_context(tc.manual_schedule())
 
         ident = keep.tile([P, P], F32, name="ident")
-        make_identity(nc, ident[:])
         warm = keep.tile([P, 8], F32, name="warm")
         nc.vector.memset(warm[:], 0.0)
+        nc.vector.memset(ident[:], 0.0)
+        make_identity(nc, ident[:], nomemset=True)
         warm_out = keep.tile([P, 8], F32, name="warm_out")
         nc.scalar.activation(out=warm_out[:], in_=warm[:], func=TANH)
 
@@ -79,12 +81,14 @@ def tile_coattentionaffinityimageside_w4_kernel(
             for g in range(g0, g1):
                 v_raw[b * PAIRS + g] = raw[:, 2 * D * (g - g0) : 2 * D * (g - g0 + 1)]
 
-        vs_col = load_vector("vs_col", v_scale.rearrange("a o k -> (a o k)"), F32)
+        vs_col = keep.tile([P, 2, 8], F32, name="vs_col")
+        nc.sync.dma_start(out=vs_col[:, :, 0:2], in_=v_scale.rearrange("a o (h p j) -> p (a o h) j", h=2, j=2))
         load_q(0, 0)
         load_v(0, 0, 1)
         load_q(0, 1)
+        load_v(0, 1, 2)
         wb_col = load_vector("wb_col", wb, BF16)
-        load_v(0, 1, PAIRS)
+        load_v(0, 2, PAIRS)
         gp_col = load_vector("gp_col", gp, BF16)
         load_weight("wq", wq_words, wq_scales)
         gc_col = load_vector("gc_col", gc, BF16)
@@ -94,19 +98,18 @@ def tile_coattentionaffinityimageside_w4_kernel(
         load_v(1, 0, PAIRS)
 
         vs_full = keep.tile([P, 2 * D], F32, name="vs_full")
-        spread = psum.tile([P, PACK, P], F32, name="spread", tag="bank", bufs=6)
-        for j in range(PACK):
-            nc.tensor.transpose(spread[:, j, :], vs_col[:, j : j + 1].to_broadcast([P, P]), ident[:])
-        nc.vector.tensor_copy(
-            out=vs_full[:, :D].rearrange("p (m j) -> p m j", j=PACK), in_=spread[:].rearrange("p j m -> p m j")
-        )
-        nc.scalar.copy(
-            out=vs_full[:, D:].rearrange("p (m j) -> p m j", j=PACK), in_=spread[:].rearrange("p j m -> p m j")
-        )
+        for h, copy in enumerate((nc.vector.tensor_copy, nc.scalar.copy)):
+            spread = psum.tile([P, 2, P], F32, name="spread", tag="bank", bufs=5)
+            for j in range(2):
+                nc.tensor.transpose(spread[:, j, :], vs_col[:, h, j : j + 1].to_broadcast([P, P]), ident[:])
+            copy(
+                out=vs_full[:, 2 * P * h : 2 * P * (h + 1)].rearrange("p (m j) -> p m j", j=2),
+                in_=spread[:].rearrange("p j m -> p m j"),
+            )
 
         def turn(rows, grouped):
             words = rows.bitcast(F32)
-            bank = psum.tile([P, 2, 2, P], F32, name="turned", tag="bank", bufs=6)
+            bank = psum.tile([P, 2, 2, P], F32, name="turned", tag="bank", bufs=5)
             for a in range(2):
                 for u in range(2):
                     nc.tensor.transpose(bank[:, a, u, :], words[:, 256 * a + u : 256 * (a + 1) : 2], ident[:])
@@ -170,7 +173,7 @@ def tile_coattentionaffinityimageside_w4_kernel(
         def project_q(b, j):
             if j == 0:
                 pq_planes[b] = work.tile([P, PACK, E], BF16, name="pq_planes", bufs=1)
-            acc = psum.tile([P, E], F32, name="pq_acc", tag="bank", bufs=6)
+            acc = psum.tile([P, E], F32, name="pq_acc", tag="bank", bufs=5)
             project(acc[:], q_mx[b], P * j, "wq")
             nc.scalar.activation(out=pq_planes[b][:, j, :], in_=acc[:], func=COPY, scale=gp_f32[:, j : j + 1])
 
@@ -184,14 +187,13 @@ def tile_coattentionaffinityimageside_w4_kernel(
         def quant_pq(b):
             pq_mx[b] = quantize("pq", pq_grp[b][:], work, 2)
 
-        def widen(s, parts):
+        def widen(s, spans):
             v_wide[s] = work.tile([P, 2 * D], BF16, name="v_wide")
-            w = 2 * D // parts
-            for i in range(parts):
+            for c0, c1 in spans:
                 nc.vector.tensor_tensor(
-                    out=v_wide[s][:, w * i : w * (i + 1)],
-                    in0=v_raw[s][:, w * i : w * (i + 1)].bitcast(FP8),
-                    in1=vs_full[:, :w],
+                    out=v_wide[s][:, c0:c1],
+                    in0=v_raw[s][:, c0:c1].bitcast(FP8),
+                    in1=vs_full[:, c0 % D : c0 % D + c1 - c0],
                     op=MULT,
                 )
 
@@ -205,7 +207,7 @@ def tile_coattentionaffinityimageside_w4_kernel(
         def affinity(s, a):
             if a == 0:
                 c_val[s] = work.tile([P, 2, P, PACK], F32, name="c_val")
-            acc = psum.tile([P, PACK, P], F32, name="score", tag="bank", bufs=6)
+            acc = psum.tile([P, PACK, P], F32, name="score", tag="bank", bufs=5)
             for j in range(PACK):
                 product(acc[:, j, :], qb_mx[s // PAIRS], P * j, v_mx[s], P * a, P)
             nc.scalar.activation(
@@ -214,49 +216,54 @@ def tile_coattentionaffinityimageside_w4_kernel(
 
         def project_v(s, a):
             if a == 0:
-                pv_val[s] = work.tile([P, 2, E], F32, name="pv_val")
-            acc = psum.tile([P, E], F32, name="pv_acc", tag="bank", bufs=6)
+                pv_val[s] = work.tile([P, 2, E], F32, name="pv_val", bufs=4)
+            acc = psum.tile([P, E], F32, name="pv_acc", tag="bank", bufs=5)
             project(acc[:], v_mx[s], P * a, "wv")
             nc.scalar.copy(out=pv_val[s][:, a, :], in_=acc[:])
 
-        def gain(s):
-            cg_val[s] = work.tile([P, 2 * P * PACK], BF16, name="cg_val", align_bytes=64)
+        def gain(s, a0, a1):
+            cols = (a1 - a0) * P
+            values = work.tile([P, cols * PACK], BF16, name="cg_val", align_bytes=64)
             nc.vector.tensor_tensor(
-                out=cg_val[s][:].rearrange("p (r j) -> p r j", j=PACK),
-                in0=c_val[s][:].rearrange("p a r j -> p (a r) j"),
-                in1=gc_col[:].unsqueeze(1).to_broadcast([P, 2 * P, PACK]),
+                out=values[:].rearrange("p (r j) -> p r j", j=PACK),
+                in0=c_val[s][:, a0:a1].rearrange("p a r j -> p (a r) j"),
+                in1=gc_col[:].unsqueeze(1).to_broadcast([P, cols, PACK]),
                 op=MULT,
             )
+            cg_val[s, a0] = values
 
-        def quant_cg(s):
-            cg_mx[s] = quantize("cg", cg_val[s][:], work, 3)
+        def quant_cg(s, a0, a1):
+            packed = quantize("cg", cg_val[s, a0][:], work, 3)
+            for a in range(a0, a1):
+                cg_mx[s, a] = (packed, P * (a - a0))
 
         def mix(s, a):
-            m_acc[s, a] = psum.tile([P, E], F32, name="m_acc", tag="mix")
-            product(m_acc[s, a][:], cg_mx[s], P * a, pq_mx[s // PAIRS], 0, E)
+            m_acc[s, a] = psum.tile([P, E], F32, name="m_acc", tag="mix", bufs=3)
+            product(m_acc[s, a][:], cg_mx[s, a][0], cg_mx[s, a][1], pq_mx[s // PAIRS], 0, E)
 
-        def add(s, a):
-            if a == 0:
-                total[s] = work.tile([P, 2, E], F32, name="total")
+        def add(s, a, c0=0, c1=E):
+            if a == 0 and c0 == 0:
+                total[s] = work.tile([P, 2 * E], F32, name="total")
             nc.vector.scalar_tensor_tensor(
-                out=total[s][:, a, :], in0=m_acc[s, a][:], scalar=1.0 / math.sqrt(T), in1=pv_val[s][:, a, :],
-                op0=MULT, op1=ADD,
+                out=total[s][:, E * a + c0 : E * a + c1], in0=m_acc[s, a][:, c0:c1], scalar=1.0 / math.sqrt(T),
+                in1=pv_val[s][:, a, c0:c1], op0=MULT, op1=ADD,
             )
 
-        def finish(s, a0, a1):
-            res = work.tile([P, a1 - a0, E], F32, name="res", bufs=4)
-            nc.scalar.activation(out=res[:], in_=total[s][:, a0:a1, :], func=TANH)
+        def finish(s, c0, c1):
+            res = work.tile([P, c1 - c0], F32, name="res", bufs=6)
+            nc.scalar.activation(out=res[:], in_=total[s][:, c0:c1], func=TANH)
             b, g = divmod(s, PAIRS)
-            dst = out[b].rearrange("(p i) e -> p i e", i=ROWS)
-            nc.sync.dma_start(out=dst[:, 2 * g + a0 : 2 * g + a1, :], in_=res[:])
+            dst = out[b].rearrange("(p i) e -> p (i e)", i=ROWS)
+            nc.sync.dma_start(out=dst[:, 2 * E * g + c0 : 2 * E * g + c1], in_=res[:])
 
+        nc.scalar.copy(out=vs_full[:, D:], in_=vs_full[:, :D])
         turn_q(0, 0)
-        widen(0, 2)
+        widen(0, [(0, 256), (512, 768), (256, 512), (768, 1024)])
         turn_q(0, 1)
         turn_v(0)
         gp_f32 = keep.tile([P, PACK], F32, name="gp_f32")
         nc.scalar.copy(out=gp_f32[:], in_=gp_col[:])
-        widen(1, 1)
+        widen(1, WHOLE)
         quant_q(0)
         scale_q(0)
         turn_v(1)
@@ -264,36 +271,36 @@ def tile_coattentionaffinityimageside_w4_kernel(
         for j in range(2):
             project_q(0, j)
         quant_qb(0)
-        widen(2, 1)
+        widen(2, WHOLE)
         for j in range(2, 4):
             project_q(0, j)
         affinity(0, 0)
         affinity(0, 1)
         quant_v(1)
-        widen(3, 1)
+        widen(3, WHOLE)
         turn_v(2)
         group_pq(0)
         affinity(1, 0)
         affinity(1, 1)
 
-        for s in range(STEPS + 1):
+        last = STEPS - 1
+        for s in range(last):
             if s + 2 < STEPS:
                 quant_v(s + 2)
-            if s < STEPS:
-                gain(s)
-            if s + 3 < STEPS:
-                turn_v(s + 3)
+            gain(s, 0, 2)
             if s == 0:
                 turn_q(1, 0)
                 turn_q(1, 1)
             if s > 0:
                 add(s - 1, 0)
-            if s % PAIRS == 0 and s < STEPS:
+            if s % PAIRS == 0:
                 quant_pq(s // PAIRS)
-            if s < STEPS:
+            if s <= PAIRS:
                 project_v(s, 0)
                 project_v(s, 1)
-                quant_cg(s)
+            if s + 3 < STEPS:
+                turn_v(s + 3)
+            quant_cg(s, 0, 2)
             if s > 0:
                 add(s - 1, 1)
             if s + 2 < STEPS:
@@ -304,19 +311,34 @@ def tile_coattentionaffinityimageside_w4_kernel(
                 project_q(1, 2 * s - 1)
             if s == 1:
                 scale_q(1)
-            if s < STEPS:
-                mix(s, 0)
-                mix(s, 1)
+            if s >= PAIRS:
+                for a in range(2):
+                    project_v(s + 1, a)
+                    finish(s - 1, E * a, E * (a + 1))
+            if 0 < s < PAIRS:
+                finish(s - 1, 0, 2 * E)
+            mix(s, 0)
+            mix(s, 1)
             if s + 4 < STEPS:
-                widen(s + 4, 1)
+                widen(s + 4, WHOLE)
             if s == 0:
                 quant_q(1)
             if s == 1:
                 quant_qb(1)
             if s == 3:
                 group_pq(1)
-            if 0 < s < STEPS:
-                finish(s - 1, 0, 2)
-            if s == STEPS:
-                finish(s - 1, 0, 1)
-                finish(s - 1, 1, 2)
+        gain(last, 0, 1)
+        add(last - 1, 0)
+        finish(last - 1, 0, E)
+        quant_cg(last, 0, 1)
+        mix(last, 0)
+        gain(last, 1, 2)
+        add(last - 1, 1)
+        finish(last - 1, E, 2 * E)
+        quant_cg(last, 1, 2)
+        mix(last, 1)
+        add(last, 0)
+        finish(last, 0, E)
+        for c0 in (0, E // 2):
+            add(last, 1, c0, c0 + E // 2)
+            finish(last, E + c0, E + c0 + E // 2)

@@ -25,6 +25,11 @@ PACK = 4
 ROWS = N // P
 PAIRS = ROWS // 2
 STEPS = B * PAIRS
+POOL_STEPS = range(0, 8)
+VEC_PV = (0, 3, 7)
+PQ_STEPS = [1, 2]
+ACT_BANKS = 4
+VEC_BANKS = 3
 WHOLE = [(0, 2 * D)]
 
 
@@ -43,6 +48,8 @@ def tile_coattentionaffinityimageside_w4_kernel(
         nc.vector.memset(warm[:], 0.0)
         nc.vector.memset(ident[:], 0.0)
         make_identity(nc, ident[:], nomemset=True)
+        ident_bf = keep.tile([P, P], BF16, name="ident_bf")
+        nc.vector.tensor_copy(out=ident_bf[:], in_=ident[:])
         warm_out = keep.tile([P, 8], F32, name="warm_out")
         nc.scalar.activation(out=warm_out[:], in_=warm[:], func=TANH)
 
@@ -88,10 +95,10 @@ def tile_coattentionaffinityimageside_w4_kernel(
         load_q(0, 1)
         load_v(0, 1, 2)
         wb_col = load_vector("wb_col", wb, BF16)
+        gc_col = load_vector("gc_col", gc, BF16)
         load_v(0, 2, PAIRS)
         gp_col = load_vector("gp_col", gp, BF16)
         load_weight("wq", wq_words, wq_scales)
-        gc_col = load_vector("gc_col", gc, BF16)
         load_weight("wv", wv_words, wv_scales)
         load_q(1, 0)
         load_q(1, 1)
@@ -99,7 +106,7 @@ def tile_coattentionaffinityimageside_w4_kernel(
 
         vs_full = keep.tile([P, 2 * D], F32, name="vs_full")
         for h, copy in enumerate((nc.vector.tensor_copy, nc.scalar.copy)):
-            spread = psum.tile([P, 2, P], F32, name="spread", tag="bank", bufs=5)
+            spread = psum.tile([P, 2, P], F32, name="spread", tag="bank", bufs=ACT_BANKS)
             for j in range(2):
                 nc.tensor.transpose(spread[:, j, :], vs_col[:, h, j : j + 1].to_broadcast([P, P]), ident[:])
             copy(
@@ -109,7 +116,7 @@ def tile_coattentionaffinityimageside_w4_kernel(
 
         def turn(rows, grouped):
             words = rows.bitcast(F32)
-            bank = psum.tile([P, 2, 2, P], F32, name="turned", tag="bank", bufs=5)
+            bank = psum.tile([P, 2, 2, P], F32, name="turned", tag="bank", bufs=ACT_BANKS)
             for a in range(2):
                 for u in range(2):
                     nc.tensor.transpose(bank[:, a, u, :], words[:, 256 * a + u : 256 * (a + 1) : 2], ident[:])
@@ -147,6 +154,7 @@ def tile_coattentionaffinityimageside_w4_kernel(
                 stop=True,
             )
 
+        pv_acc = {}
         q_grp, qb_grp, q_mx, qb_mx, pq_planes, pq_grp, pq_mx = {}, {}, {}, {}, {}, {}, {}
         v_wide, v_grp, v_mx, c_val, cg_val, cg_mx, pv_val, m_acc, total = {}, {}, {}, {}, {}, {}, {}, {}, {}
 
@@ -173,7 +181,7 @@ def tile_coattentionaffinityimageside_w4_kernel(
         def project_q(b, j):
             if j == 0:
                 pq_planes[b] = work.tile([P, PACK, E], BF16, name="pq_planes", bufs=1)
-            acc = psum.tile([P, E], F32, name="pq_acc", tag="bank", bufs=5)
+            acc = psum.tile([P, E], F32, name="pq_acc", tag="bank", bufs=ACT_BANKS)
             project(acc[:], q_mx[b], P * j, "wq")
             nc.scalar.activation(out=pq_planes[b][:, j, :], in_=acc[:], func=COPY, scale=gp_f32[:, j : j + 1])
 
@@ -207,38 +215,36 @@ def tile_coattentionaffinityimageside_w4_kernel(
         def affinity(s, a):
             if a == 0:
                 c_val[s] = work.tile([P, 2, P, PACK], F32, name="c_val")
-            acc = psum.tile([P, PACK, P], F32, name="score", tag="bank", bufs=5)
+            acc = psum.tile([P, PACK, P], F32, name="score", tag="bank", bufs=ACT_BANKS)
             for j in range(PACK):
                 product(acc[:, j, :], qb_mx[s // PAIRS], P * j, v_mx[s], P * a, P)
             nc.scalar.activation(
                 out=c_val[s][:, a, :, :], in_=acc[:].rearrange("p j r -> p r j"), func=TANH, scale=1.0 / math.sqrt(D)
             )
 
-        def project_v(s, a):
+        def project_v(s, a, tag="bank", bufs=ACT_BANKS):
             if a == 0:
                 pv_val[s] = work.tile([P, 2, E], F32, name="pv_val", bufs=4)
-            acc = psum.tile([P, E], F32, name="pv_acc", tag="bank", bufs=5)
-            project(acc[:], v_mx[s], P * a, "wv")
-            nc.scalar.copy(out=pv_val[s][:, a, :], in_=acc[:])
+            pv_acc[s, a] = psum.tile([P, E], F32, name="pv_acc", tag=tag, bufs=bufs)
+            project(pv_acc[s, a][:], v_mx[s], P * a, "wv")
 
-        def gain(s, a0, a1):
-            cols = (a1 - a0) * P
-            values = work.tile([P, cols * PACK], BF16, name="cg_val", align_bytes=64)
-            nc.vector.tensor_tensor(
-                out=values[:].rearrange("p (r j) -> p r j", j=PACK),
-                in0=c_val[s][:, a0:a1].rearrange("p a r j -> p (a r) j"),
-                in1=gc_col[:].unsqueeze(1).to_broadcast([P, cols, PACK]),
-                op=MULT,
-            )
-            cg_val[s, a0] = values
+        def empty_pv(s, a, copy):
+            copy(out=pv_val[s][:, a, :], in_=pv_acc[s, a][:])
 
-        def quant_cg(s, a0, a1):
-            packed = quantize("cg", cg_val[s, a0][:], work, 3)
-            for a in range(a0, a1):
-                cg_mx[s, a] = (packed, P * (a - a0))
+        def gain(s, a):
+            values = work.tile([P, P * PACK], BF16, name="cg_val_%d" % a, bufs=2 - a, align_bytes=64)
+            tanh_values = c_val[s][:, a].rearrange("p r j -> p (r j)")
+            if a == 0 or s not in POOL_STEPS:
+                nc.vector.tensor_tensor(out=values[:], in0=tanh_values, in1=gc_bank[:], op=MULT)
+            else:
+                nc.gpsimd.tensor_tensor(out=values[:], in0=tanh_values, in1=gc_full[:], op=MULT)
+            cg_val[s, a] = values
+
+        def quant_cg(s, a):
+            cg_mx[s, a] = (quantize("cg", cg_val[s, a][:], work, 4), 0)
 
         def mix(s, a):
-            m_acc[s, a] = psum.tile([P, E], F32, name="m_acc", tag="mix", bufs=3)
+            m_acc[s, a] = psum.tile([P, E], F32, name="m_acc", tag="mix", bufs=VEC_BANKS)
             product(m_acc[s, a][:], cg_mx[s, a][0], cg_mx[s, a][1], pq_mx[s // PAIRS], 0, E)
 
         def add(s, a, c0=0, c1=E):
@@ -264,6 +270,10 @@ def tile_coattentionaffinityimageside_w4_kernel(
         gp_f32 = keep.tile([P, PACK], F32, name="gp_f32")
         nc.scalar.copy(out=gp_f32[:], in_=gp_col[:])
         widen(1, WHOLE)
+        gc_full = keep.tile([P, P * PACK], BF16, name="gc_full")
+        nc.vector.tensor_copy(
+            out=gc_full[:].rearrange("p (r j) -> p r j", j=PACK), in_=gc_col[:].unsqueeze(1).to_broadcast([P, P, PACK])
+        )
         quant_q(0)
         scale_q(0)
         turn_v(1)
@@ -276,67 +286,72 @@ def tile_coattentionaffinityimageside_w4_kernel(
             project_q(0, j)
         affinity(0, 0)
         affinity(0, 1)
+        gc_bank = psum.tile([P, P * PACK], F32, name="gc_bank", bufs=1)
+        nc.tensor.matmul(gc_bank[:], lhsT=ident_bf[:], rhs=gc_full[:], start=True, stop=True)
         quant_v(1)
-        widen(3, WHOLE)
         turn_v(2)
-        group_pq(0)
-        affinity(1, 0)
-        affinity(1, 1)
 
         last = STEPS - 1
-        for s in range(last):
-            if s + 2 < STEPS:
-                quant_v(s + 2)
-            gain(s, 0, 2)
+        for s in range(STEPS):
+            if s + 3 < STEPS:
+                widen(s + 3, WHOLE)
+            if s > 0:
+                quant_cg(s - 1, 0)
+            if s % PAIRS == 1:
+                quant_pq(s // PAIRS)
+            if s + 1 < STEPS:
+                affinity(s + 1, 0)
+                affinity(s + 1, 1)
+            if 1 < s <= PAIRS + 1:
+                finish(s - 2, 0, 2 * E)
+            if s > PAIRS + 1:
+                finish(s - 2, E, 2 * E)
+            project_v(s, 0)
+            empty_pv(s, 0, nc.scalar.copy)
+            if s in VEC_PV:
+                project_v(s, 1, "mix", VEC_BANKS)
+            else:
+                project_v(s, 1)
+                empty_pv(s, 1, nc.scalar.copy)
             if s == 0:
                 turn_q(1, 0)
                 turn_q(1, 1)
-            if s > 0:
-                add(s - 1, 0)
-            if s % PAIRS == 0:
-                quant_pq(s // PAIRS)
-            if s <= PAIRS:
-                project_v(s, 0)
-                project_v(s, 1)
             if s + 3 < STEPS:
                 turn_v(s + 3)
-            quant_cg(s, 0, 2)
             if s > 0:
-                add(s - 1, 1)
-            if s + 2 < STEPS:
-                affinity(s + 2, 0)
-                affinity(s + 2, 1)
-            if s in (1, 2):
-                project_q(1, 2 * s - 2)
-                project_q(1, 2 * s - 1)
+                mix(s - 1, 0)
             if s == 1:
-                scale_q(1)
-            if s >= PAIRS:
-                for a in range(2):
-                    project_v(s + 1, a)
-                    finish(s - 1, E * a, E * (a + 1))
-            if 0 < s < PAIRS:
-                finish(s - 1, 0, 2 * E)
-            mix(s, 0)
-            mix(s, 1)
-            if s + 4 < STEPS:
-                widen(s + 4, WHOLE)
-            if s == 0:
                 quant_q(1)
-            if s == 1:
+            if s == 2:
+                scale_q(1)
+            if s % PAIRS == 0:
+                group_pq(s // PAIRS)
+            if s + 2 < STEPS:
+                quant_v(s + 2)
+            if s == 2:
                 quant_qb(1)
-            if s == 3:
-                group_pq(1)
-        gain(last, 0, 1)
-        add(last - 1, 0)
-        finish(last - 1, 0, E)
-        quant_cg(last, 0, 1)
-        mix(last, 0)
-        gain(last, 1, 2)
-        add(last - 1, 1)
-        finish(last - 1, E, 2 * E)
-        quant_cg(last, 1, 2)
+            if s > 0:
+                quant_cg(s - 1, 1)
+            gain(s, 1)
+            gain(s, 0)
+            if s > 0:
+                mix(s - 1, 1)
+            if s in PQ_STEPS:
+                project_q(1, 2 * PQ_STEPS.index(s))
+                project_q(1, 2 * PQ_STEPS.index(s) + 1)
+            if s in VEC_PV:
+                empty_pv(s, 1, nc.vector.tensor_copy)
+            if s > 0:
+                add(s - 1, 0)
+                if s == last:
+                    quant_cg(last, 0)
+                    mix(last, 0)
+                if s > PAIRS:
+                    finish(s - 1, 0, E)
+                add(s - 1, 1)
+        quant_cg(last, 1)
         mix(last, 1)
+        finish(last - 1, E, 2 * E)
         add(last, 0)
         finish(last, 0, E)
         for c0 in (0, E // 2):

@@ -22,15 +22,12 @@ COPY = mybir.ActivationFunctionType.Copy
 
 P = 128
 PACK = 4
-ROWS = N // P
-PAIRS = ROWS // 2
+TILES = N // P
+PAIRS = TILES // 2
 STEPS = B * PAIRS
-POOL_STEPS = range(0, 8)
-VEC_PV = (0, 3, 7)
-PQ_STEPS = [1, 2]
-ACT_BANKS = 4
-VEC_BANKS = 3
-WHOLE = [(0, 2 * D)]
+LAST = STEPS - 1
+SCALAR_BANKS = 4
+VECTOR_BANKS = 3
 
 
 def tile_coattentionaffinityimageside_w4_kernel(
@@ -40,128 +37,115 @@ def tile_coattentionaffinityimageside_w4_kernel(
     with ExitStack() as ctx:
         keep = ctx.enter_context(tc.tile_pool(name="keep", bufs=1))
         work = ctx.enter_context(tc.tile_pool(name="work", bufs=3))
-        psum = ctx.enter_context(tc.psum_pool(name="psum", bufs=2))
+        psum = ctx.enter_context(tc.psum_pool(name="psum", bufs=1))
         ctx.enter_context(tc.manual_schedule())
 
+        def scalar_bank(name, shape):
+            return psum.tile(shape, F32, name=name, tag="scalar_banks", bufs=SCALAR_BANKS)
+
+        def vector_bank(name, shape):
+            return psum.tile(shape, F32, name=name, tag="vector_banks", bufs=VECTOR_BANKS)
+
         ident = keep.tile([P, P], F32, name="ident")
-        warm = keep.tile([P, 8], F32, name="warm")
-        nc.vector.memset(warm[:], 0.0)
         nc.vector.memset(ident[:], 0.0)
         make_identity(nc, ident[:], nomemset=True)
         ident_bf = keep.tile([P, P], BF16, name="ident_bf")
         nc.vector.tensor_copy(out=ident_bf[:], in_=ident[:])
-        warm_out = keep.tile([P, 8], F32, name="warm_out")
-        nc.scalar.activation(out=warm_out[:], in_=warm[:], func=TANH)
 
-        w_codes = {}
-        w_scale = {}
+        w_codes, w_scale = {}, {}
         for name in ("wq", "wv"):
             w_scale[name] = keep.tile([P, E], U8, name=name + "_scale", align_bytes=64)
             nc.vector.memset(w_scale[name][:].bitcast(I32), 0)
-
-        def load_vector(name, vec, dtype):
-            col = keep.tile([P, PACK], dtype, name=name)
-            nc.sync.dma_start(out=col[:], in_=vec.rearrange("(p j) -> p j", j=PACK))
-            return col
 
         def load_weight(name, words, scales):
             w_codes[name] = keep.tile([P, 2 * E], U8, name=name + "_codes", align_bytes=64)
             nc.sync.dma_start(out=w_codes[name][:].bitcast(I32), in_=words[0].bitcast(I32))
             for r in range(4):
-                nc.sync.dma_start(
-                    out=w_scale[name][r:P:32, :].bitcast(I32), in_=scales[0, r:16:4, :].bitcast(I32)
-                )
+                nc.sync.dma_start(out=w_scale[name][r:P:32, :].bitcast(I32), in_=scales[0, r:16:4, :].bitcast(I32))
 
-        q_rows = {}
+        def load_vector(name, vec):
+            col = keep.tile([P, PACK], BF16, name=name)
+            nc.sync.dma_start(out=col[:], in_=vec.rearrange("(p j) -> p j", j=PACK))
+            return col
 
-        def load_q(b, h):
-            q_rows[b, h] = keep.tile([P, 2 * D], BF16, name="q_rows_%d_%d" % (b, h))
-            src = q[b].rearrange("(m j) k -> m (j k)", j=PACK)
-            nc.sync.dma_start(out=q_rows[b, h][:], in_=src[:, 2 * D * h : 2 * D * (h + 1)])
+        q_rows, v_raw = {}, {}
 
-        v_raw = {}
+        def load_q(b, half):
+            q_rows[b, half] = keep.tile([P, 2 * D], BF16, name="q_rows_%d_%d" % (b, half))
+            src = q[b].rearrange("(p j) k -> p (j k)", j=PACK)
+            nc.sync.dma_start(out=q_rows[b, half][:], in_=src[:, 2 * D * half : 2 * D * (half + 1)])
 
-        def load_v(b, g0, g1):
-            raw = keep.tile([P, 2 * D * (g1 - g0)], U8, name="v_raw_%d_%d" % (b, g0))
-            src = v_bytes[b].rearrange("(p i) k -> p (i k)", i=ROWS)
-            nc.sync.dma_start(out=raw[:], in_=src[:, 2 * D * g0 : 2 * D * g1])
-            for g in range(g0, g1):
-                v_raw[b * PAIRS + g] = raw[:, 2 * D * (g - g0) : 2 * D * (g - g0 + 1)]
+        def load_v(s0, s1):
+            b, g0 = divmod(s0, PAIRS)
+            raw = keep.tile([P, 2 * D * (s1 - s0)], U8, name="v_raw_%d" % s0)
+            src = v_bytes[b].rearrange("(p i) k -> p (i k)", i=TILES)
+            nc.sync.dma_start(out=raw[:], in_=src[:, 2 * D * g0 : 2 * D * (g0 + s1 - s0)])
+            for s in range(s0, s1):
+                v_raw[s] = raw[:, 2 * D * (s - s0) : 2 * D * (s - s0 + 1)]
 
         vs_col = keep.tile([P, 2, 8], F32, name="vs_col")
         nc.sync.dma_start(out=vs_col[:, :, 0:2], in_=v_scale.rearrange("a o (h p j) -> p (a o h) j", h=2, j=2))
         load_q(0, 0)
-        load_v(0, 0, 1)
+        load_v(0, 1)
         load_q(0, 1)
-        load_v(0, 1, 2)
-        wb_col = load_vector("wb_col", wb, BF16)
-        gc_col = load_vector("gc_col", gc, BF16)
-        load_v(0, 2, PAIRS)
-        gp_col = load_vector("gp_col", gp, BF16)
+        load_v(1, 2)
+        wb_col = load_vector("wb_col", wb)
+        gc_col = load_vector("gc_col", gc)
+        load_v(2, PAIRS)
+        gp_col = load_vector("gp_col", gp)
         load_weight("wq", wq_words, wq_scales)
         load_weight("wv", wv_words, wv_scales)
         load_q(1, 0)
         load_q(1, 1)
-        load_v(1, 0, PAIRS)
+        load_v(PAIRS, STEPS)
 
         vs_full = keep.tile([P, 2 * D], F32, name="vs_full")
-        for h, copy in enumerate((nc.vector.tensor_copy, nc.scalar.copy)):
-            spread = psum.tile([P, 2, P], F32, name="spread", tag="bank", bufs=ACT_BANKS)
+        for half, copy in enumerate((nc.vector.tensor_copy, nc.scalar.copy)):
+            spread = scalar_bank("spread", [P, 2, P])
             for j in range(2):
-                nc.tensor.transpose(spread[:, j, :], vs_col[:, h, j : j + 1].to_broadcast([P, P]), ident[:])
+                nc.tensor.transpose(spread[:, j, :], vs_col[:, half, j : j + 1].to_broadcast([P, P]), ident[:])
             copy(
-                out=vs_full[:, 2 * P * h : 2 * P * (h + 1)].rearrange("p (m j) -> p m j", j=2),
+                out=vs_full[:, 2 * P * half : 2 * P * (half + 1)].rearrange("p (m j) -> p m j", j=2),
                 in_=spread[:].rearrange("p j m -> p m j"),
             )
+        nc.scalar.copy(out=vs_full[:, D:], in_=vs_full[:, :D])
 
         def turn(rows, grouped):
             words = rows.bitcast(F32)
-            bank = psum.tile([P, 2, 2, P], F32, name="turned", tag="bank", bufs=ACT_BANKS)
+            bank = scalar_bank("turned", [P, 2, 2, P])
             for a in range(2):
                 for u in range(2):
-                    nc.tensor.transpose(bank[:, a, u, :], words[:, 256 * a + u : 256 * (a + 1) : 2], ident[:])
+                    nc.tensor.transpose(bank[:, a, u, :], words[:, 2 * P * a + u : 2 * P * (a + 1) : 2], ident[:])
             nc.scalar.copy(
                 out=grouped.bitcast(F32).rearrange("p (a r u) -> p a r u", a=2, u=2),
                 in_=bank[:].rearrange("p a u r -> p a r u"),
             )
 
-        def quantize(name, values, pool, bufs):
-            cols = values.shape[1] // PACK
-            codes = pool.tile([P, cols], U32, name=name + "_codes", bufs=bufs, align_bytes=64)
-            scales = pool.tile([P, cols], U8, name=name + "_scales", bufs=bufs, align_bytes=64)
-            nc.vector.quantize_mx(out=codes[:].bitcast(FP8X4), scales=scales[:], in_=values)
+        def quantize(name, grouped, bufs):
+            cols = grouped.shape[1] // PACK
+            codes = work.tile([P, cols], U32, name=name + "_codes", bufs=bufs, align_bytes=64)
+            scales = work.tile([P, cols], U8, name=name + "_scales", bufs=bufs, align_bytes=64)
+            nc.vector.quantize_mx(out=codes[:].bitcast(FP8X4), scales=scales[:], in_=grouped)
             return codes, scales
 
-        def product(acc, left, c0, right, r0, width):
+        def mx_pass(acc, left, c0, rhs, rhs_scale):
+            codes, scales = left
             nc.tensor.matmul_mx(
                 out=acc,
-                lhsT=left[0][:, c0 : c0 + P].bitcast(FP8X4),
-                lhsT_scale=left[1][:, c0 : c0 + P],
-                rhs=right[0][:, r0 : r0 + width].bitcast(FP8X4),
-                rhs_scale=right[1][:, r0 : r0 + width],
+                lhsT=codes[:, c0 : c0 + P].bitcast(FP8X4),
+                lhsT_scale=scales[:, c0 : c0 + P],
+                rhs=rhs,
+                rhs_scale=rhs_scale,
                 start=True,
                 stop=True,
             )
 
-        def project(acc, left, c0, name):
-            nc.tensor.matmul_mx(
-                out=acc,
-                lhsT=left[0][:, c0 : c0 + P].bitcast(FP8X4),
-                lhsT_scale=left[1][:, c0 : c0 + P],
-                rhs=w_codes[name][:].bitcast(FP4X4),
-                rhs_scale=w_scale[name][:],
-                start=True,
-                stop=True,
-            )
+        q_grp, qb_grp, q_mx, qb_mx, pq_rows, pq_grp, pq_mx = {}, {}, {}, {}, {}, {}, {}
 
-        pv_acc = {}
-        q_grp, qb_grp, q_mx, qb_mx, pq_planes, pq_grp, pq_mx = {}, {}, {}, {}, {}, {}, {}
-        v_wide, v_grp, v_mx, c_val, cg_val, cg_mx, pv_val, m_acc, total = {}, {}, {}, {}, {}, {}, {}, {}, {}
-
-        def turn_q(b, h):
-            if h == 0:
+        def turn_q(b, half):
+            if half == 0:
                 q_grp[b] = work.tile([P, PACK * T], BF16, name="q_grp", bufs=1, align_bytes=64)
-            turn(q_rows[b, h][:], q_grp[b][:, 2 * D * h : 2 * D * (h + 1)])
+            turn(q_rows[b, half][:], q_grp[b][:, 2 * D * half : 2 * D * (half + 1)])
 
         def scale_q(b):
             qb_grp[b] = work.tile([P, PACK * T], BF16, name="qb_grp", bufs=1, align_bytes=64)
@@ -172,30 +156,33 @@ def tile_coattentionaffinityimageside_w4_kernel(
                 op=MULT,
             )
 
-        def quant_q(b):
-            q_mx[b] = quantize("q", q_grp[b][:], work, 2)
+        def quantize_q(b):
+            q_mx[b] = quantize("q", q_grp[b][:], B)
 
-        def quant_qb(b):
-            qb_mx[b] = quantize("qb", qb_grp[b][:], work, 2)
+        def quantize_qb(b):
+            qb_mx[b] = quantize("qb", qb_grp[b][:], B)
 
         def project_q(b, j):
             if j == 0:
-                pq_planes[b] = work.tile([P, PACK, E], BF16, name="pq_planes", bufs=1)
-            acc = psum.tile([P, E], F32, name="pq_acc", tag="bank", bufs=ACT_BANKS)
-            project(acc[:], q_mx[b], P * j, "wq")
-            nc.scalar.activation(out=pq_planes[b][:, j, :], in_=acc[:], func=COPY, scale=gp_f32[:, j : j + 1])
+                pq_rows[b] = work.tile([P, PACK, E], BF16, name="pq_rows", bufs=1)
+            acc = scalar_bank("pq_acc", [P, E])
+            mx_pass(acc[:], q_mx[b], P * j, w_codes["wq"][:].bitcast(FP4X4), w_scale["wq"][:])
+            nc.scalar.activation(out=pq_rows[b][:, j, :], in_=acc[:], func=COPY, scale=gp_f32[:, j : j + 1])
 
         def group_pq(b):
             pq_grp[b] = work.tile([P, PACK * E], BF16, name="pq_grp", bufs=1, align_bytes=64)
             nc.vector.tensor_copy(
                 out=pq_grp[b][:].rearrange("p (c i j) -> p c j i", i=4, j=PACK),
-                in_=pq_planes[b][:].rearrange("p j (c i) -> p c j i", i=4),
+                in_=pq_rows[b][:].rearrange("p j (c i) -> p c j i", i=4),
             )
 
-        def quant_pq(b):
-            pq_mx[b] = quantize("pq", pq_grp[b][:], work, 2)
+        def quantize_pq(b):
+            pq_mx[b] = quantize("pq", pq_grp[b][:], B)
 
-        def widen(s, spans):
+        v_wide, v_grp, v_mx, c_val, cg_grp, cg_mx = {}, {}, {}, {}, {}, {}
+        pv_acc, pv_val, m_acc, total = {}, {}, {}, {}
+
+        def widen(s, spans=((0, 2 * D),)):
             v_wide[s] = work.tile([P, 2 * D], BF16, name="v_wide")
             for c0, c1 in spans:
                 nc.vector.tensor_tensor(
@@ -209,151 +196,156 @@ def tile_coattentionaffinityimageside_w4_kernel(
             v_grp[s] = work.tile([P, 2 * D], BF16, name="v_grp", align_bytes=64)
             turn(v_wide[s][:], v_grp[s][:])
 
-        def quant_v(s):
-            v_mx[s] = quantize("v", v_grp[s][:], work, 3)
+        def quantize_v(s):
+            v_mx[s] = quantize("v", v_grp[s][:], 3)
 
-        def affinity(s, a):
-            if a == 0:
-                c_val[s] = work.tile([P, 2, P, PACK], F32, name="c_val")
-            acc = psum.tile([P, PACK, P], F32, name="score", tag="bank", bufs=ACT_BANKS)
-            for j in range(PACK):
-                product(acc[:, j, :], qb_mx[s // PAIRS], P * j, v_mx[s], P * a, P)
-            nc.scalar.activation(
-                out=c_val[s][:, a, :, :], in_=acc[:].rearrange("p j r -> p r j"), func=TANH, scale=1.0 / math.sqrt(D)
-            )
+        def affinity(s):
+            c_val[s] = work.tile([P, 2, P, PACK], F32, name="c_val")
+            codes, scales = v_mx[s]
+            for a in range(2):
+                acc = scalar_bank("score", [P, PACK, P])
+                cols = slice(P * a, P * (a + 1))
+                for j in range(PACK):
+                    mx_pass(acc[:, j, :], qb_mx[s // PAIRS], P * j, codes[:, cols].bitcast(FP8X4), scales[:, cols])
+                nc.scalar.activation(
+                    out=c_val[s][:, a, :, :],
+                    in_=acc[:].rearrange("p j r -> p r j"),
+                    func=TANH,
+                    scale=1.0 / math.sqrt(D),
+                )
 
-        def project_v(s, a, tag="bank", bufs=ACT_BANKS):
+        def project_v(s, a, bank):
             if a == 0:
                 pv_val[s] = work.tile([P, 2, E], F32, name="pv_val", bufs=4)
-            pv_acc[s, a] = psum.tile([P, E], F32, name="pv_acc", tag=tag, bufs=bufs)
-            project(pv_acc[s, a][:], v_mx[s], P * a, "wv")
+            pv_acc[s, a] = bank("pv_acc", [P, E])
+            mx_pass(pv_acc[s, a][:], v_mx[s], P * a, w_codes["wv"][:].bitcast(FP4X4), w_scale["wv"][:])
 
         def empty_pv(s, a, copy):
             copy(out=pv_val[s][:, a, :], in_=pv_acc[s, a][:])
 
-        def gain(s, a):
-            values = work.tile([P, P * PACK], BF16, name="cg_val_%d" % a, bufs=2 - a, align_bytes=64)
-            tanh_values = c_val[s][:, a].rearrange("p r j -> p (r j)")
-            if a == 0 or s not in POOL_STEPS:
-                nc.vector.tensor_tensor(out=values[:], in0=tanh_values, in1=gc_bank[:], op=MULT)
-            else:
-                nc.gpsimd.tensor_tensor(out=values[:], in0=tanh_values, in1=gc_full[:], op=MULT)
-            cg_val[s, a] = values
+        def gain(s):
+            cg_grp[s, 1] = work.tile([P, P * PACK], BF16, name="cg_grp_gpsimd", bufs=1, align_bytes=64)
+            nc.gpsimd.tensor_tensor(
+                out=cg_grp[s, 1][:], in0=c_val[s][:, 1].rearrange("p r j -> p (r j)"), in1=gc_full[:], op=MULT
+            )
+            cg_grp[s, 0] = work.tile([P, P * PACK], BF16, name="cg_grp_vector", bufs=2, align_bytes=64)
+            nc.vector.tensor_tensor(
+                out=cg_grp[s, 0][:], in0=c_val[s][:, 0].rearrange("p r j -> p (r j)"), in1=gc_bank[:], op=MULT
+            )
 
-        def quant_cg(s, a):
-            cg_mx[s, a] = (quantize("cg", cg_val[s, a][:], work, 4), 0)
+        def quantize_cg(s, a):
+            cg_mx[s, a] = quantize("cg", cg_grp[s, a][:], 4)
 
         def mix(s, a):
-            m_acc[s, a] = psum.tile([P, E], F32, name="m_acc", tag="mix", bufs=VEC_BANKS)
-            product(m_acc[s, a][:], cg_mx[s, a][0], cg_mx[s, a][1], pq_mx[s // PAIRS], 0, E)
+            m_acc[s, a] = vector_bank("m_acc", [P, E])
+            codes, scales = pq_mx[s // PAIRS]
+            mx_pass(m_acc[s, a][:], cg_mx[s, a], 0, codes[:].bitcast(FP8X4), scales[:])
 
-        def add(s, a, c0=0, c1=E):
-            if a == 0 and c0 == 0:
+        def add(s, a, e0=0, e1=E):
+            if a == 0:
                 total[s] = work.tile([P, 2 * E], F32, name="total")
             nc.vector.scalar_tensor_tensor(
-                out=total[s][:, E * a + c0 : E * a + c1], in0=m_acc[s, a][:, c0:c1], scalar=1.0 / math.sqrt(T),
-                in1=pv_val[s][:, a, c0:c1], op0=MULT, op1=ADD,
+                out=total[s][:, E * a + e0 : E * a + e1],
+                in0=m_acc[s, a][:, e0:e1],
+                scalar=1.0 / math.sqrt(T),
+                in1=pv_val[s][:, a, e0:e1],
+                op0=MULT,
+                op1=ADD,
             )
 
         def finish(s, c0, c1):
             res = work.tile([P, c1 - c0], F32, name="res", bufs=6)
             nc.scalar.activation(out=res[:], in_=total[s][:, c0:c1], func=TANH)
             b, g = divmod(s, PAIRS)
-            dst = out[b].rearrange("(p i) e -> p (i e)", i=ROWS)
+            dst = out[b].rearrange("(p i) e -> p (i e)", i=TILES)
             nc.sync.dma_start(out=dst[:, 2 * E * g + c0 : 2 * E * g + c1], in_=res[:])
 
-        nc.scalar.copy(out=vs_full[:, D:], in_=vs_full[:, :D])
         turn_q(0, 0)
-        widen(0, [(0, 256), (512, 768), (256, 512), (768, 1024)])
+        widen(0, [(D * a + D // 2 * half, D * a + D // 2 * (half + 1)) for half in range(2) for a in range(2)])
         turn_q(0, 1)
         turn_v(0)
         gp_f32 = keep.tile([P, PACK], F32, name="gp_f32")
         nc.scalar.copy(out=gp_f32[:], in_=gp_col[:])
-        widen(1, WHOLE)
+        widen(1)
         gc_full = keep.tile([P, P * PACK], BF16, name="gc_full")
         nc.vector.tensor_copy(
             out=gc_full[:].rearrange("p (r j) -> p r j", j=PACK), in_=gc_col[:].unsqueeze(1).to_broadcast([P, P, PACK])
         )
-        quant_q(0)
+        quantize_q(0)
         scale_q(0)
         turn_v(1)
-        quant_v(0)
-        for j in range(2):
-            project_q(0, j)
-        quant_qb(0)
-        widen(2, WHOLE)
-        for j in range(2, 4):
-            project_q(0, j)
-        affinity(0, 0)
-        affinity(0, 1)
-        gc_bank = psum.tile([P, P * PACK], F32, name="gc_bank", bufs=1)
+        quantize_v(0)
+        project_q(0, 0)
+        project_q(0, 1)
+        quantize_qb(0)
+        widen(2)
+        project_q(0, 2)
+        project_q(0, 3)
+        affinity(0)
+        gc_bank = psum.tile([P, P * PACK], F32, name="gc_bank")
         nc.tensor.matmul(gc_bank[:], lhsT=ident_bf[:], rhs=gc_full[:], start=True, stop=True)
-        quant_v(1)
+        quantize_v(1)
         turn_v(2)
 
-        last = STEPS - 1
         for s in range(STEPS):
+            vector_pv = s == 0 or s % PAIRS == PAIRS - 1
+            by_tile = s > PAIRS
             if s + 3 < STEPS:
-                widen(s + 3, WHOLE)
+                widen(s + 3)
             if s > 0:
-                quant_cg(s - 1, 0)
+                quantize_cg(s - 1, 0)
             if s % PAIRS == 1:
-                quant_pq(s // PAIRS)
+                quantize_pq(s // PAIRS)
             if s + 1 < STEPS:
-                affinity(s + 1, 0)
-                affinity(s + 1, 1)
-            if 1 < s <= PAIRS + 1:
-                finish(s - 2, 0, 2 * E)
-            if s > PAIRS + 1:
-                finish(s - 2, E, 2 * E)
-            project_v(s, 0)
+                affinity(s + 1)
+            if s > 1:
+                finish(s - 2, E if s - 1 > PAIRS else 0, 2 * E)
+            project_v(s, 0, scalar_bank)
             empty_pv(s, 0, nc.scalar.copy)
-            if s in VEC_PV:
-                project_v(s, 1, "mix", VEC_BANKS)
-            else:
-                project_v(s, 1)
+            project_v(s, 1, vector_bank if vector_pv else scalar_bank)
+            if not vector_pv:
                 empty_pv(s, 1, nc.scalar.copy)
             if s == 0:
                 turn_q(1, 0)
                 turn_q(1, 1)
-            if s + 3 < STEPS:
-                turn_v(s + 3)
             if s > 0:
                 mix(s - 1, 0)
+            if s + 3 < STEPS:
+                turn_v(s + 3)
             if s == 1:
-                quant_q(1)
+                quantize_q(1)
             if s == 2:
                 scale_q(1)
             if s % PAIRS == 0:
                 group_pq(s // PAIRS)
             if s + 2 < STEPS:
-                quant_v(s + 2)
+                quantize_v(s + 2)
             if s == 2:
-                quant_qb(1)
+                quantize_qb(1)
             if s > 0:
-                quant_cg(s - 1, 1)
-            gain(s, 1)
-            gain(s, 0)
+                quantize_cg(s - 1, 1)
+            gain(s)
             if s > 0:
                 mix(s - 1, 1)
-            if s in PQ_STEPS:
-                project_q(1, 2 * PQ_STEPS.index(s))
-                project_q(1, 2 * PQ_STEPS.index(s) + 1)
-            if s in VEC_PV:
+            if s in (1, 2):
+                project_q(1, 2 * s - 2)
+                project_q(1, 2 * s - 1)
+            if vector_pv:
                 empty_pv(s, 1, nc.vector.tensor_copy)
             if s > 0:
                 add(s - 1, 0)
-                if s == last:
-                    quant_cg(last, 0)
-                    mix(last, 0)
-                if s > PAIRS:
+                if s == LAST:
+                    quantize_cg(LAST, 0)
+                    mix(LAST, 0)
+                if by_tile:
                     finish(s - 1, 0, E)
                 add(s - 1, 1)
-        quant_cg(last, 1)
-        mix(last, 1)
-        finish(last - 1, E, 2 * E)
-        add(last, 0)
-        finish(last, 0, E)
-        for c0 in (0, E // 2):
-            add(last, 1, c0, c0 + E // 2)
-            finish(last, E + c0, E + c0 + E // 2)
+
+        quantize_cg(LAST, 1)
+        mix(LAST, 1)
+        finish(LAST - 1, E, 2 * E)
+        add(LAST, 0)
+        finish(LAST, 0, E)
+        for e0 in (0, E // 2):
+            add(LAST, 1, e0, e0 + E // 2)
+            finish(LAST, E + e0, E + e0 + E // 2)

import math
from contextlib import ExitStack

import concourse.mybir as mybir
from concourse.masks import make_identity

B, N, T, D, E = 2, 1024, 512, 512, 512
FLOPS = 2 * B * (T * N * D + N * D * E + T * D * E + N * T * E)

F32 = mybir.dt.float32
BF16 = mybir.dt.bfloat16
U8 = mybir.dt.uint8
U32 = mybir.dt.uint32
I32 = mybir.dt.int32
FP8 = mybir.dt.float8_e4m3fn
FP8X4 = mybir.dt.float8_e4m3fn_x4
FP4X4 = mybir.dt.float4_e2m1fn_x4
MULT = mybir.AluOpType.mult
ADD = mybir.AluOpType.add
TANH = mybir.ActivationFunctionType.Tanh
COPY = mybir.ActivationFunctionType.Copy

P = 128
PACK = 4
TILES = N // P
PAIRS = TILES // 2
STEPS = B * PAIRS
LAST = STEPS - 1
SCALAR_BANKS = 4
VECTOR_BANKS = 3


def tile_coattentionaffinityimageside_w4_kernel(
    tc, v_bytes, v_scale, q, wb, wv_words, wv_scales, wq_words, wq_scales, gc, gp, out
):
    nc = tc.nc
    with ExitStack() as ctx:
        keep = ctx.enter_context(tc.tile_pool(name="keep", bufs=1))
        work = ctx.enter_context(tc.tile_pool(name="work", bufs=3))
        psum = ctx.enter_context(tc.psum_pool(name="psum", bufs=1))
        ctx.enter_context(tc.manual_schedule())

        def scalar_bank(name, shape):
            return psum.tile(shape, F32, name=name, tag="scalar_banks", bufs=SCALAR_BANKS)

        def vector_bank(name, shape):
            return psum.tile(shape, F32, name=name, tag="vector_banks", bufs=VECTOR_BANKS)

        ident = keep.tile([P, P], F32, name="ident")
        nc.vector.memset(ident[:], 0.0)
        make_identity(nc, ident[:], nomemset=True)
        ident_bf = keep.tile([P, P], BF16, name="ident_bf")
        nc.vector.tensor_copy(out=ident_bf[:], in_=ident[:])

        w_codes, w_scale = {}, {}
        for name in ("wq", "wv"):
            w_scale[name] = keep.tile([P, E], U8, name=name + "_scale", align_bytes=64)
            nc.vector.memset(w_scale[name][:].bitcast(I32), 0)

        def load_weight(name, words, scales):
            w_codes[name] = keep.tile([P, 2 * E], U8, name=name + "_codes", align_bytes=64)
            nc.sync.dma_start(out=w_codes[name][:].bitcast(I32), in_=words[0].bitcast(I32))
            for r in range(4):
                nc.sync.dma_start(out=w_scale[name][r:P:32, :].bitcast(I32), in_=scales[0, r:16:4, :].bitcast(I32))

        def load_vector(name, vec):
            col = keep.tile([P, PACK], BF16, name=name)
            nc.sync.dma_start(out=col[:], in_=vec.rearrange("(p j) -> p j", j=PACK))
            return col

        q_rows, v_raw = {}, {}

        def load_q(b, half):
            q_rows[b, half] = keep.tile([P, 2 * D], BF16, name="q_rows_%d_%d" % (b, half))
            src = q[b].rearrange("(p j) k -> p (j k)", j=PACK)
            nc.sync.dma_start(out=q_rows[b, half][:], in_=src[:, 2 * D * half : 2 * D * (half + 1)])

        def load_v(s0, s1):
            b, g0 = divmod(s0, PAIRS)
            raw = keep.tile([P, 2 * D * (s1 - s0)], U8, name="v_raw_%d" % s0)
            src = v_bytes[b].rearrange("(p i) k -> p (i k)", i=TILES)
            nc.sync.dma_start(out=raw[:], in_=src[:, 2 * D * g0 : 2 * D * (g0 + s1 - s0)])
            for s in range(s0, s1):
                v_raw[s] = raw[:, 2 * D * (s - s0) : 2 * D * (s - s0 + 1)]

        vs_col = keep.tile([P, 2, 8], F32, name="vs_col")
        nc.sync.dma_start(out=vs_col[:, :, 0:2], in_=v_scale.rearrange("a o (h p j) -> p (a o h) j", h=2, j=2))
        load_q(0, 0)
        load_v(0, 1)
        load_q(0, 1)
        load_v(1, 2)
        wb_col = load_vector("wb_col", wb)
        gc_col = load_vector("gc_col", gc)
        load_v(2, PAIRS)
        gp_col = load_vector("gp_col", gp)
        load_weight("wq", wq_words, wq_scales)
        load_weight("wv", wv_words, wv_scales)
        load_q(1, 0)
        load_q(1, 1)
        load_v(PAIRS, STEPS)

        vs_full = keep.tile([P, 2 * D], F32, name="vs_full")
        for half, copy in enumerate((nc.vector.tensor_copy, nc.scalar.copy)):
            spread = scalar_bank("spread", [P, 2, P])
            for j in range(2):
                nc.tensor.transpose(spread[:, j, :], vs_col[:, half, j : j + 1].to_broadcast([P, P]), ident[:])
            copy(
                out=vs_full[:, 2 * P * half : 2 * P * (half + 1)].rearrange("p (m j) -> p m j", j=2),
                in_=spread[:].rearrange("p j m -> p m j"),
            )
        nc.scalar.copy(out=vs_full[:, D:], in_=vs_full[:, :D])

        def turn(rows, grouped):
            words = rows.bitcast(F32)
            bank = scalar_bank("turned", [P, 2, 2, P])
            for a in range(2):
                for u in range(2):
                    nc.tensor.transpose(bank[:, a, u, :], words[:, 2 * P * a + u : 2 * P * (a + 1) : 2], ident[:])
            nc.scalar.copy(
                out=grouped.bitcast(F32).rearrange("p (a r u) -> p a r u", a=2, u=2),
                in_=bank[:].rearrange("p a u r -> p a r u"),
            )

        def quantize(name, grouped, bufs):
            cols = grouped.shape[1] // PACK
            codes = work.tile([P, cols], U32, name=name + "_codes", bufs=bufs, align_bytes=64)
            scales = work.tile([P, cols], U8, name=name + "_scales", bufs=bufs, align_bytes=64)
            nc.vector.quantize_mx(out=codes[:].bitcast(FP8X4), scales=scales[:], in_=grouped)
            return codes, scales

        def mx_pass(acc, left, c0, rhs, rhs_scale):
            codes, scales = left
            nc.tensor.matmul_mx(
                out=acc,
                lhsT=codes[:, c0 : c0 + P].bitcast(FP8X4),
                lhsT_scale=scales[:, c0 : c0 + P],
                rhs=rhs,
                rhs_scale=rhs_scale,
                start=True,
                stop=True,
            )

        q_grp, qb_grp, q_mx, qb_mx, pq_rows, pq_grp, pq_mx = {}, {}, {}, {}, {}, {}, {}

        def turn_q(b, half):
            if half == 0:
                q_grp[b] = work.tile([P, PACK * T], BF16, name="q_grp", bufs=1, align_bytes=64)
            turn(q_rows[b, half][:], q_grp[b][:, 2 * D * half : 2 * D * (half + 1)])

        def scale_q(b):
            qb_grp[b] = work.tile([P, PACK * T], BF16, name="qb_grp", bufs=1, align_bytes=64)
            nc.vector.tensor_tensor(
                out=qb_grp[b][:].rearrange("p (t j) -> p t j", j=PACK),
                in0=q_grp[b][:].rearrange("p (t j) -> p t j", j=PACK),
                in1=wb_col[:].unsqueeze(1).to_broadcast([P, T, PACK]),
                op=MULT,
            )

        def quantize_q(b):
            q_mx[b] = quantize("q", q_grp[b][:], B)

        def quantize_qb(b):
            qb_mx[b] = quantize("qb", qb_grp[b][:], B)

        def project_q(b, j):
            if j == 0:
                pq_rows[b] = work.tile([P, PACK, E], BF16, name="pq_rows", bufs=1)
            acc = scalar_bank("pq_acc", [P, E])
            mx_pass(acc[:], q_mx[b], P * j, w_codes["wq"][:].bitcast(FP4X4), w_scale["wq"][:])
            nc.scalar.activation(out=pq_rows[b][:, j, :], in_=acc[:], func=COPY, scale=gp_f32[:, j : j + 1])

        def group_pq(b):
            pq_grp[b] = work.tile([P, PACK * E], BF16, name="pq_grp", bufs=1, align_bytes=64)
            nc.vector.tensor_copy(
                out=pq_grp[b][:].rearrange("p (c i j) -> p c j i", i=4, j=PACK),
                in_=pq_rows[b][:].rearrange("p j (c i) -> p c j i", i=4),
            )

        def quantize_pq(b):
            pq_mx[b] = quantize("pq", pq_grp[b][:], B)

        v_wide, v_grp, v_mx, c_val, cg_grp, cg_mx = {}, {}, {}, {}, {}, {}
        pv_acc, pv_val, m_acc, total = {}, {}, {}, {}

        def widen(s, spans=((0, 2 * D),)):
            v_wide[s] = work.tile([P, 2 * D], BF16, name="v_wide")
            for c0, c1 in spans:
                nc.vector.tensor_tensor(
                    out=v_wide[s][:, c0:c1],
                    in0=v_raw[s][:, c0:c1].bitcast(FP8),
                    in1=vs_full[:, c0 % D : c0 % D + c1 - c0],
                    op=MULT,
                )

        def turn_v(s):
            v_grp[s] = work.tile([P, 2 * D], BF16, name="v_grp", align_bytes=64)
            turn(v_wide[s][:], v_grp[s][:])

        def quantize_v(s):
            v_mx[s] = quantize("v", v_grp[s][:], 3)

        def affinity(s):
            c_val[s] = work.tile([P, 2, P, PACK], F32, name="c_val")
            codes, scales = v_mx[s]
            for a in range(2):
                acc = scalar_bank("score", [P, PACK, P])
                cols = slice(P * a, P * (a + 1))
                for j in range(PACK):
                    mx_pass(acc[:, j, :], qb_mx[s // PAIRS], P * j, codes[:, cols].bitcast(FP8X4), scales[:, cols])
                nc.scalar.activation(
                    out=c_val[s][:, a, :, :],
                    in_=acc[:].rearrange("p j r -> p r j"),
                    func=TANH,
                    scale=1.0 / math.sqrt(D),
                )

        def project_v(s, a, bank):
            if a == 0:
                pv_val[s] = work.tile([P, 2, E], F32, name="pv_val", bufs=4)
            pv_acc[s, a] = bank("pv_acc", [P, E])
            mx_pass(pv_acc[s, a][:], v_mx[s], P * a, w_codes["wv"][:].bitcast(FP4X4), w_scale["wv"][:])

        def empty_pv(s, a, copy):
            copy(out=pv_val[s][:, a, :], in_=pv_acc[s, a][:])

        def gain(s):
            cg_grp[s, 1] = work.tile([P, P * PACK], BF16, name="cg_grp_gpsimd", bufs=1, align_bytes=64)
            nc.gpsimd.tensor_tensor(
                out=cg_grp[s, 1][:], in0=c_val[s][:, 1].rearrange("p r j -> p (r j)"), in1=gc_full[:], op=MULT
            )
            cg_grp[s, 0] = work.tile([P, P * PACK], BF16, name="cg_grp_vector", bufs=2, align_bytes=64)
            nc.vector.tensor_tensor(
                out=cg_grp[s, 0][:], in0=c_val[s][:, 0].rearrange("p r j -> p (r j)"), in1=gc_bank[:], op=MULT
            )

        def quantize_cg(s, a):
            cg_mx[s, a] = quantize("cg", cg_grp[s, a][:], 4)

        def mix(s, a):
            m_acc[s, a] = vector_bank("m_acc", [P, E])
            codes, scales = pq_mx[s // PAIRS]
            mx_pass(m_acc[s, a][:], cg_mx[s, a], 0, codes[:].bitcast(FP8X4), scales[:])

        def add(s, a, e0=0, e1=E):
            if a == 0:
                total[s] = work.tile([P, 2 * E], F32, name="total")
            nc.vector.scalar_tensor_tensor(
                out=total[s][:, E * a + e0 : E * a + e1],
                in0=m_acc[s, a][:, e0:e1],
                scalar=1.0 / math.sqrt(T),
                in1=pv_val[s][:, a, e0:e1],
                op0=MULT,
                op1=ADD,
            )

        def finish(s, c0, c1):
            res = work.tile([P, c1 - c0], F32, name="res", bufs=6)
            nc.scalar.activation(out=res[:], in_=total[s][:, c0:c1], func=TANH)
            b, g = divmod(s, PAIRS)
            dst = out[b].rearrange("(p i) e -> p (i e)", i=TILES)
            nc.sync.dma_start(out=dst[:, 2 * E * g + c0 : 2 * E * g + c1], in_=res[:])

        turn_q(0, 0)
        widen(0, [(D * a + D // 2 * half, D * a + D // 2 * (half + 1)) for half in range(2) for a in range(2)])
        turn_q(0, 1)
        turn_v(0)
        gp_f32 = keep.tile([P, PACK], F32, name="gp_f32")
        nc.scalar.copy(out=gp_f32[:], in_=gp_col[:])
        widen(1)
        gc_full = keep.tile([P, P * PACK], BF16, name="gc_full")
        nc.vector.tensor_copy(
            out=gc_full[:].rearrange("p (r j) -> p r j", j=PACK), in_=gc_col[:].unsqueeze(1).to_broadcast([P, P, PACK])
        )
        quantize_q(0)
        scale_q(0)
        turn_v(1)
        quantize_v(0)
        project_q(0, 0)
        project_q(0, 1)
        quantize_qb(0)
        widen(2)
        project_q(0, 2)
        project_q(0, 3)
        affinity(0)
        gc_bank = psum.tile([P, P * PACK], F32, name="gc_bank")
        nc.tensor.matmul(gc_bank[:], lhsT=ident_bf[:], rhs=gc_full[:], start=True, stop=True)
        quantize_v(1)
        turn_v(2)

        for s in range(STEPS):
            vector_pv = s == 0 or s % PAIRS == PAIRS - 1
            by_tile = s > PAIRS
            if s + 3 < STEPS:
                widen(s + 3)
            if s > 0:
                quantize_cg(s - 1, 0)
            if s % PAIRS == 1:
                quantize_pq(s // PAIRS)
            if s + 1 < STEPS:
                affinity(s + 1)
            if s > 1:
                finish(s - 2, E if s - 1 > PAIRS else 0, 2 * E)
            project_v(s, 0, scalar_bank)
            empty_pv(s, 0, nc.scalar.copy)
            project_v(s, 1, vector_bank if vector_pv else scalar_bank)
            if not vector_pv:
                empty_pv(s, 1, nc.scalar.copy)
            if s == 0:
                turn_q(1, 0)
                turn_q(1, 1)
            if s > 0:
                mix(s - 1, 0)
            if s + 3 < STEPS:
                turn_v(s + 3)
            if s == 1:
                quantize_q(1)
            if s == 2:
                scale_q(1)
            if s % PAIRS == 0:
                group_pq(s // PAIRS)
            if s + 2 < STEPS:
                quantize_v(s + 2)
            if s == 2:
                quantize_qb(1)
            if s > 0:
                quantize_cg(s - 1, 1)
            gain(s)
            if s > 0:
                mix(s - 1, 1)
            if s in (1, 2):
                project_q(1, 2 * s - 2)
                project_q(1, 2 * s - 1)
            if vector_pv:
                empty_pv(s, 1, nc.vector.tensor_copy)
            if s > 0:
                add(s - 1, 0)
                if s == LAST:
                    quantize_cg(LAST, 0)
                    mix(LAST, 0)
                if by_tile:
                    finish(s - 1, 0, E)
                add(s - 1, 1)

        quantize_cg(LAST, 1)
        mix(LAST, 1)
        finish(LAST - 1, E, 2 * E)
        add(LAST, 0)
        finish(LAST, 0, E)
        for e0 in (0, E // 2):
            add(LAST, 1, e0, e0 + E // 2)
            finish(LAST, E + e0, E + e0 + E // 2)
